import numpy as np
import ml_dtypes

BF16 = ml_dtypes.bfloat16


def bf(x):
    return np.asarray(x, np.float32).astype(BF16)


def f32(x):
    return np.asarray(x, np.float32)


def f64(x):
    return np.asarray(x).astype(np.float64)


def striped(idx):
    return np.tile(idx.reshape(-1, 16).T, (8, 1))


S, K, M, N, H = 2048, 128, 512, 384, 256


def sigmoid(v):
    return 1.0 / (1.0 + np.exp(-v))


def setup_inputs():
    return {"table": bf(np.random.standard_normal((K, S))), "w": bf(np.random.standard_normal((K, M)) / np.sqrt(K)), "offs": striped(np.random.permutation(np.tile(np.arange(S), 2))[:N])}


def reference(table, w, offs):
    idx = offs[:16].T.reshape(-1)
    x = f64(table)[:, idx]
    y = f64(w).T @ x
    return y[:H] * sigmoid(y[H:])

@@ -1,0 +1,57 @@
+import concourse.mybir as mybir
+
+BF16 = mybir.dt.bfloat16
+F32 = mybir.dt.float32
+U16 = mybir.dt.uint16
+SIGMOID = mybir.ActivationFunctionType.Sigmoid
+MULT = mybir.AluOpType.mult
+
+P = 128
+S = 2048
+N = 384
+M = 512
+H = 256
+
+FLOPS = 2 * P * M * N
+
+
+def tile_gather_matmul_kernel(tc, table, w, offs, out):
+    nc = tc.nc
+    with (
+        tc.tile_pool(name="held", bufs=1) as held,
+        tc.tile_pool(name="work", bufs=2) as work,
+        tc.psum_pool(name="psum", bufs=2) as psum,
+    ):
+        offsets = held.tile([P, N // 16], U16, name="offsets")
+        nc.sync.dma_start(offsets[:], offs)
+        words = held.tile([P, S], BF16, name="words")
+        nc.scalar.dma_start(words[:], table)
+        weights = held.tile([P, M], BF16, name="weights")
+        nc.sync.dma_start(weights[:], w)
+
+        for block in range(H // P):
+            rows = slice(block * P, (block + 1) * P)
+            gate_columns = slice(H + block * P, H + (block + 1) * P)
+
+            gate_bank = psum.tile([P, N], F32, name="gate_bank")
+            nc.tensor.matmul(
+                gate_bank[:],
+                weights[:, gate_columns],
+                words[:].indirect(offsets[:]),
+                start=True,
+                stop=True,
+            )
+            value_bank = psum.tile([P, N], F32, name="value_bank")
+            nc.tensor.matmul(
+                value_bank[:],
+                weights[:, rows],
+                words[:].indirect(offsets[:]),
+                start=True,
+                stop=True,
+            )
+
+            gate = work.tile([P, N], F32, name="gate")
+            nc.scalar.activation(gate[:], gate_bank[:], SIGMOID)
+            gated = work.tile([P, N], F32, name="gated")
+            nc.vector.tensor_tensor(gated[:], value_bank[:], gate[:], MULT)
+            nc.sync.dma_start(out[rows, :], gated[:])

@@ -11,16 +11,19 @@ S = 2048
 N = 384
 M = 512
 H = 256
+WARM_UP_COLUMNS = 256
+WARM_UP_MATMULS = 10
 
 FLOPS = 2 * P * M * N
 
 
 def tile_gather_matmul_kernel(tc, table, w, offs, out):
     nc = tc.nc
+    blocks = range(H // P)
     with (
         tc.tile_pool(name="held", bufs=1) as held,
-        tc.tile_pool(name="work", bufs=2) as work,
-        tc.psum_pool(name="psum", bufs=2) as psum,
+        tc.tile_pool(name="work", bufs=len(blocks)) as work,
+        tc.psum_pool(name="psum", bufs=len(blocks)) as psum,
     ):
         offsets = held.tile([P, N // 16], U16, name="offsets")
         nc.sync.dma_start(offsets[:], offs)
@@ -29,18 +32,28 @@ def tile_gather_matmul_kernel(tc, table, w, offs, out):
         weights = held.tile([P, M], BF16, name="weights")
         nc.sync.dma_start(weights[:], w)
 
-        for block in range(H // P):
-            rows = slice(block * P, (block + 1) * P)
-            gate_columns = slice(H + block * P, H + (block + 1) * P)
+        zeros = held.tile([P, WARM_UP_COLUMNS], BF16, name="zeros")
+        nc.vector.memset(zeros[:], 0.0)
+        unread_bank = psum.tile([P, WARM_UP_COLUMNS], F32, name="unread_bank", bufs=1)
+        for warm in range(WARM_UP_MATMULS):
+            nc.tensor.matmul(unread_bank[:], zeros[:, :P], zeros[:], start=True, stop=True)
 
+        gates = []
+        for block in blocks:
             gate_bank = psum.tile([P, N], F32, name="gate_bank")
             nc.tensor.matmul(
                 gate_bank[:],
-                weights[:, gate_columns],
+                weights[:, H + block * P : H + (block + 1) * P],
                 words[:].indirect(offsets[:]),
                 start=True,
                 stop=True,
             )
+            gate = work.tile([P, N], F32, name="gate")
+            nc.scalar.activation(gate[:], gate_bank[:], SIGMOID)
+            gates.append(gate)
+
+        for block in blocks:
+            rows = slice(block * P, (block + 1) * P)
             value_bank = psum.tile([P, N], F32, name="value_bank")
             nc.tensor.matmul(
                 value_bank[:],
@@ -49,9 +62,6 @@ def tile_gather_matmul_kernel(tc, table, w, offs, out):
                 start=True,
                 stop=True,
             )
-
-            gate = work.tile([P, N], F32, name="gate")
-            nc.scalar.activation(gate[:], gate_bank[:], SIGMOID)
             gated = work.tile([P, N], F32, name="gated")
-            nc.vector.tensor_tensor(gated[:], value_bank[:], gate[:], MULT)
+            nc.vector.tensor_tensor(gated[:], value_bank[:], gates[block][:], MULT)
             nc.sync.dma_start(out[rows, :], gated[:])

@@ -11,8 +11,6 @@ S = 2048
 N = 384
 M = 512
 H = 256
-WARM_UP_COLUMNS = 256
-WARM_UP_MATMULS = 10
 
 FLOPS = 2 * P * M * N
 
@@ -32,11 +30,10 @@ def tile_gather_matmul_kernel(tc, table, w, offs, out):
         weights = held.tile([P, M], BF16, name="weights")
         nc.sync.dma_start(weights[:], w)
 
-        zeros = held.tile([P, WARM_UP_COLUMNS], BF16, name="zeros")
-        nc.vector.memset(zeros[:], 0.0)
-        unread_bank = psum.tile([P, WARM_UP_COLUMNS], F32, name="unread_bank", bufs=1)
-        for warm in range(WARM_UP_MATMULS):
-            nc.tensor.matmul(unread_bank[:], zeros[:, :P], zeros[:], start=True, stop=True)
+        early_in = held.tile([P, 1], F32, name="early_in")
+        nc.vector.memset(early_in[:], 0.0)
+        early_out = held.tile([P, 1], F32, name="early_out")
+        nc.scalar.activation(early_out[:], early_in[:], SIGMOID)
 
         gates = []
         for block in blocks:

@@ -11,6 +11,7 @@ S = 2048
 N = 384
 M = 512
 H = 256
+PIECE = N // 2
 
 FLOPS = 2 * P * M * N
 
@@ -18,6 +19,7 @@ FLOPS = 2 * P * M * N
 def tile_gather_matmul_kernel(tc, table, w, offs, out):
     nc = tc.nc
     blocks = range(H // P)
+    pieces = range(N // PIECE)
     with (
         tc.tile_pool(name="held", bufs=1) as held,
         tc.tile_pool(name="work", bufs=len(blocks)) as work,
@@ -51,14 +53,17 @@ def tile_gather_matmul_kernel(tc, table, w, offs, out):
 
         for block in blocks:
             rows = slice(block * P, (block + 1) * P)
-            value_bank = psum.tile([P, N], F32, name="value_bank")
-            nc.tensor.matmul(
-                value_bank[:],
-                weights[:, rows],
-                words[:].indirect(offsets[:]),
-                start=True,
-                stop=True,
-            )
-            gated = work.tile([P, N], F32, name="gated")
-            nc.vector.tensor_tensor(gated[:], value_bank[:], gates[block][:], MULT)
-            nc.sync.dma_start(out[rows, :], gated[:])
+            for piece in pieces:
+                columns = slice(piece * PIECE, (piece + 1) * PIECE)
+                piece_offsets = offsets[:, piece * PIECE // 16 : (piece + 1) * PIECE // 16]
+                value_bank = psum.tile([P, PIECE], F32, name="value_bank", bufs=len(blocks) * len(pieces))
+                nc.tensor.matmul(
+                    value_bank[:],
+                    weights[:, rows],
+                    words[:].indirect(piece_offsets),
+                    start=True,
+                    stop=True,
+                )
+                gated = work.tile([P, PIECE], F32, name="gated", bufs=len(blocks) * len(pieces))
+                nc.vector.tensor_tensor(gated[:], value_bank[:], gates[block][:, columns], MULT)
+                nc.sync.dma_start(out[rows, columns], gated[:])

@@ -37,7 +37,7 @@ def tile_gather_matmul_kernel(tc, table, w, offs, out):
         early_out = held.tile([P, 1], F32, name="early_out")
         nc.scalar.activation(early_out[:], early_in[:], SIGMOID)
 
-        gates = []
+        gates = {}
         for block in blocks:
             gate_bank = psum.tile([P, N], F32, name="gate_bank")
             nc.tensor.matmul(
@@ -47,9 +47,10 @@ def tile_gather_matmul_kernel(tc, table, w, offs, out):
                 start=True,
                 stop=True,
             )
-            gate = work.tile([P, N], F32, name="gate")
-            nc.scalar.activation(gate[:], gate_bank[:], SIGMOID)
-            gates.append(gate)
+            for piece in pieces:
+                gate = work.tile([P, PIECE], F32, name="gate", bufs=len(blocks) * len(pieces))
+                nc.scalar.activation(gate[:], gate_bank[:, piece * PIECE : (piece + 1) * PIECE], SIGMOID)
+                gates[block, piece] = gate
 
         for block in blocks:
             rows = slice(block * P, (block + 1) * P)
@@ -65,5 +66,5 @@ def tile_gather_matmul_kernel(tc, table, w, offs, out):
                     stop=True,
                 )
                 gated = work.tile([P, PIECE], F32, name="gated", bufs=len(blocks) * len(pieces))
-                nc.vector.tensor_tensor(gated[:], value_bank[:], gates[block][:, columns], MULT)
+                nc.vector.tensor_tensor(gated[:], value_bank[:], gates[block, piece][:], MULT)
                 nc.sync.dma_start(out[rows, columns], gated[:])

@@ -37,8 +37,7 @@ def tile_gather_matmul_kernel(tc, table, w, offs, out):
         early_out = held.tile([P, 1], F32, name="early_out")
         nc.scalar.activation(early_out[:], early_in[:], SIGMOID)
 
-        gates = {}
-        for block in blocks:
+        def make_gates(block):
             gate_bank = psum.tile([P, N], F32, name="gate_bank")
             nc.tensor.matmul(
                 gate_bank[:],
@@ -52,19 +51,26 @@ def tile_gather_matmul_kernel(tc, table, w, offs, out):
                 nc.scalar.activation(gate[:], gate_bank[:, piece * PIECE : (piece + 1) * PIECE], SIGMOID)
                 gates[block, piece] = gate
 
-        for block in blocks:
+        def make_output(block, piece):
             rows = slice(block * P, (block + 1) * P)
-            for piece in pieces:
-                columns = slice(piece * PIECE, (piece + 1) * PIECE)
-                piece_offsets = offsets[:, piece * PIECE // 16 : (piece + 1) * PIECE // 16]
-                value_bank = psum.tile([P, PIECE], F32, name="value_bank", bufs=len(blocks) * len(pieces))
-                nc.tensor.matmul(
-                    value_bank[:],
-                    weights[:, rows],
-                    words[:].indirect(piece_offsets),
-                    start=True,
-                    stop=True,
-                )
-                gated = work.tile([P, PIECE], F32, name="gated", bufs=len(blocks) * len(pieces))
-                nc.vector.tensor_tensor(gated[:], value_bank[:], gates[block, piece][:], MULT)
-                nc.sync.dma_start(out[rows, columns], gated[:])
+            columns = slice(piece * PIECE, (piece + 1) * PIECE)
+            piece_offsets = offsets[:, piece * PIECE // 16 : (piece + 1) * PIECE // 16]
+            value_bank = psum.tile([P, PIECE], F32, name="value_bank", bufs=len(blocks) * len(pieces))
+            nc.tensor.matmul(
+                value_bank[:],
+                weights[:, rows],
+                words[:].indirect(piece_offsets),
+                start=True,
+                stop=True,
+            )
+            gated = work.tile([P, PIECE], F32, name="gated", bufs=len(blocks) * len(pieces))
+            nc.vector.tensor_tensor(gated[:], value_bank[:], gates[block, piece][:], MULT)
+            nc.sync.dma_start(out[rows, columns], gated[:])
+
+        gates = {}
+        make_gates(0)
+        make_output(0, 0)
+        make_gates(1)
+        make_output(0, 1)
+        make_output(1, 0)
+        make_output(1, 1)

@@ -25,12 +25,12 @@ def tile_gather_matmul_kernel(tc, table, w, offs, out):
         tc.tile_pool(name="work", bufs=len(blocks)) as work,
         tc.psum_pool(name="psum", bufs=len(blocks)) as psum,
     ):
-        offsets = held.tile([P, N // 16], U16, name="offsets")
-        nc.sync.dma_start(offsets[:], offs)
         words = held.tile([P, S], BF16, name="words")
         nc.scalar.dma_start(words[:], table)
         weights = held.tile([P, M], BF16, name="weights")
         nc.sync.dma_start(weights[:], w)
+        offsets = held.tile([P, N // 16], U16, name="offsets")
+        nc.sync.dma_start(offsets[:], offs)
 
         early_in = held.tile([P, 1], F32, name="early_in")
         nc.vector.memset(early_in[:], 0.0)

@@ -12,6 +12,7 @@ N = 384
 M = 512
 H = 256
 PIECE = N // 2
+GATE_MATMULS = 3
 
 FLOPS = 2 * P * M * N
 
@@ -37,18 +38,20 @@ def tile_gather_matmul_kernel(tc, table, w, offs, out):
         early_out = held.tile([P, 1], F32, name="early_out")
         nc.scalar.activation(early_out[:], early_in[:], SIGMOID)
 
-        def make_gates(block):
-            gate_bank = psum.tile([P, N], F32, name="gate_bank")
+        def make_gates(block, gate_pieces):
+            first = gate_pieces[0] * PIECE
+            width = len(gate_pieces) * PIECE
+            gate_bank = psum.tile([P, width], F32, name="gate_bank", bufs=GATE_MATMULS)
             nc.tensor.matmul(
                 gate_bank[:],
                 weights[:, H + block * P : H + (block + 1) * P],
-                words[:].indirect(offsets[:]),
+                words[:].indirect(offsets[:, first // 16 : (first + width) // 16]),
                 start=True,
                 stop=True,
             )
-            for piece in pieces:
+            for place, piece in enumerate(gate_pieces):
                 gate = work.tile([P, PIECE], F32, name="gate", bufs=len(blocks) * len(pieces))
-                nc.scalar.activation(gate[:], gate_bank[:, piece * PIECE : (piece + 1) * PIECE], SIGMOID)
+                nc.scalar.activation(gate[:], gate_bank[:, place * PIECE : (place + 1) * PIECE], SIGMOID)
                 gates[block, piece] = gate
 
         def make_output(block, piece):
@@ -68,9 +71,10 @@ def tile_gather_matmul_kernel(tc, table, w, offs, out):
             nc.sync.dma_start(out[rows, columns], gated[:])
 
         gates = {}
-        make_gates(0)
+        make_gates(0, (0, 1))
         make_output(0, 0)
-        make_gates(1)
+        make_gates(1, (0,))
         make_output(0, 1)
+        make_gates(1, (1,))
         make_output(1, 0)
         make_output(1, 1)

@@ -13,6 +13,8 @@ M = 512
 H = 256
 PIECE = N // 2
 GATE_MATMULS = 3
+FIRST_BLOCK = 1
+OTHER_BLOCK = 0
 
 FLOPS = 2 * P * M * N
 
@@ -28,10 +30,17 @@ def tile_gather_matmul_kernel(tc, table, w, offs, out):
     ):
         words = held.tile([P, S], BF16, name="words")
         nc.scalar.dma_start(words[:], table)
-        weights = held.tile([P, M], BF16, name="weights")
-        nc.sync.dma_start(weights[:], w)
+        first_weights = held.tile([P, P], BF16, name="first_weights")
+        nc.sync.dma_start(first_weights[:], w[:, M - P : M])
         offsets = held.tile([P, N // 16], U16, name="offsets")
         nc.sync.dma_start(offsets[:], offs)
+        other_weights = held.tile([P, M - P], BF16, name="other_weights")
+        nc.scalar.dma_start(other_weights[:], w[:, 0 : M - P])
+
+        def gate_weights(block):
+            if block == FIRST_BLOCK:
+                return first_weights[:]
+            return other_weights[:, H + block * P : H + (block + 1) * P]
 
         early_in = held.tile([P, 1], F32, name="early_in")
         nc.vector.memset(early_in[:], 0.0)
@@ -44,7 +53,7 @@ def tile_gather_matmul_kernel(tc, table, w, offs, out):
             gate_bank = psum.tile([P, width], F32, name="gate_bank", bufs=GATE_MATMULS)
             nc.tensor.matmul(
                 gate_bank[:],
-                weights[:, H + block * P : H + (block + 1) * P],
+                gate_weights(block),
                 words[:].indirect(offsets[:, first // 16 : (first + width) // 16]),
                 start=True,
                 stop=True,
@@ -61,7 +70,7 @@ def tile_gather_matmul_kernel(tc, table, w, offs, out):
             value_bank = psum.tile([P, PIECE], F32, name="value_bank", bufs=len(blocks) * len(pieces))
             nc.tensor.matmul(
                 value_bank[:],
-                weights[:, rows],
+                other_weights[:, rows],
                 words[:].indirect(piece_offsets),
                 start=True,
                 stop=True,
@@ -71,10 +80,10 @@ def tile_gather_matmul_kernel(tc, table, w, offs, out):
             nc.sync.dma_start(out[rows, columns], gated[:])
 
         gates = {}
-        make_gates(0, (0, 1))
-        make_output(0, 0)
-        make_gates(1, (0,))
-        make_output(0, 1)
-        make_gates(1, (1,))
-        make_output(1, 0)
-        make_output(1, 1)
+        make_gates(FIRST_BLOCK, (0, 1))
+        make_output(FIRST_BLOCK, 0)
+        make_gates(OTHER_BLOCK, (0,))
+        make_output(FIRST_BLOCK, 1)
+        make_gates(OTHER_BLOCK, (1,))
+        make_output(OTHER_BLOCK, 0)
+        make_output(OTHER_BLOCK, 1)

@@ -12,7 +12,7 @@ N = 384
 M = 512
 H = 256
 PIECE = N // 2
-GATE_MATMULS = 3
+BANKS = 3
 FIRST_BLOCK = 1
 OTHER_BLOCK = 0
 
@@ -50,7 +50,7 @@ def tile_gather_matmul_kernel(tc, table, w, offs, out):
         def make_gates(block, gate_pieces):
             first = gate_pieces[0] * PIECE
             width = len(gate_pieces) * PIECE
-            gate_bank = psum.tile([P, width], F32, name="gate_bank", bufs=GATE_MATMULS)
+            gate_bank = psum.tile([P, width], F32, name="gate_bank", bufs=BANKS)
             nc.tensor.matmul(
                 gate_bank[:],
                 gate_weights(block),
@@ -63,27 +63,29 @@ def tile_gather_matmul_kernel(tc, table, w, offs, out):
                 nc.scalar.activation(gate[:], gate_bank[:, place * PIECE : (place + 1) * PIECE], SIGMOID)
                 gates[block, piece] = gate
 
-        def make_output(block, piece):
+        def make_output(block, value_pieces):
             rows = slice(block * P, (block + 1) * P)
-            columns = slice(piece * PIECE, (piece + 1) * PIECE)
-            piece_offsets = offsets[:, piece * PIECE // 16 : (piece + 1) * PIECE // 16]
-            value_bank = psum.tile([P, PIECE], F32, name="value_bank", bufs=len(blocks) * len(pieces))
+            first = value_pieces[0] * PIECE
+            width = len(value_pieces) * PIECE
+            value_bank = psum.tile([P, width], F32, name="value_bank", bufs=BANKS)
             nc.tensor.matmul(
                 value_bank[:],
                 other_weights[:, rows],
-                words[:].indirect(piece_offsets),
+                words[:].indirect(offsets[:, first // 16 : (first + width) // 16]),
                 start=True,
                 stop=True,
             )
-            gated = work.tile([P, PIECE], F32, name="gated", bufs=len(blocks) * len(pieces))
-            nc.vector.tensor_tensor(gated[:], value_bank[:], gates[block, piece][:], MULT)
-            nc.sync.dma_start(out[rows, columns], gated[:])
+            for place, piece in enumerate(value_pieces):
+                gated = work.tile([P, PIECE], F32, name="gated", bufs=len(blocks) * len(pieces))
+                nc.vector.tensor_tensor(
+                    gated[:], value_bank[:, place * PIECE : (place + 1) * PIECE], gates[block, piece][:], MULT
+                )
+                nc.sync.dma_start(out[rows, piece * PIECE : (piece + 1) * PIECE], gated[:])
 
         gates = {}
         make_gates(FIRST_BLOCK, (0, 1))
-        make_output(FIRST_BLOCK, 0)
+        make_output(FIRST_BLOCK, (0, 1))
         make_gates(OTHER_BLOCK, (0,))
-        make_output(FIRST_BLOCK, 1)
         make_gates(OTHER_BLOCK, (1,))
-        make_output(OTHER_BLOCK, 0)
-        make_output(OTHER_BLOCK, 1)
+        make_output(OTHER_BLOCK, (0,))
+        make_output(OTHER_BLOCK, (1,))

@@ -12,6 +12,7 @@ N = 384
 M = 512
 H = 256
 PIECE = N // 2
+DMA_BLOCK = 256
 BANKS = 3
 FIRST_BLOCK = 1
 OTHER_BLOCK = 0
@@ -28,13 +29,13 @@ def tile_gather_matmul_kernel(tc, table, w, offs, out):
         tc.tile_pool(name="work", bufs=len(blocks)) as work,
         tc.psum_pool(name="psum", bufs=len(blocks)) as psum,
     ):
-        words = held.tile([P, S], BF16, name="words")
+        words = held.tile([P, S], BF16, name="words", align_bytes=DMA_BLOCK)
         nc.scalar.dma_start(words[:], table)
-        first_weights = held.tile([P, P], BF16, name="first_weights")
+        first_weights = held.tile([P, P], BF16, name="first_weights", align_bytes=DMA_BLOCK)
         nc.sync.dma_start(first_weights[:], w[:, M - P : M])
         offsets = held.tile([P, N // 16], U16, name="offsets")
         nc.sync.dma_start(offsets[:], offs)
-        other_weights = held.tile([P, M - P], BF16, name="other_weights")
+        other_weights = held.tile([P, M - P], BF16, name="other_weights", align_bytes=DMA_BLOCK)
         nc.scalar.dma_start(other_weights[:], w[:, 0 : M - P])
 
         def gate_weights(block):
@@ -76,7 +77,9 @@ def tile_gather_matmul_kernel(tc, table, w, offs, out):
                 stop=True,
             )
             for place, piece in enumerate(value_pieces):
-                gated = work.tile([P, PIECE], F32, name="gated", bufs=len(blocks) * len(pieces))
+                gated = work.tile(
+                    [P, PIECE], F32, name="gated", bufs=len(blocks) * len(pieces), align_bytes=DMA_BLOCK
+                )
                 nc.vector.tensor_tensor(
                     gated[:], value_bank[:, place * PIECE : (place + 1) * PIECE], gates[block, piece][:], MULT
                 )

import concourse.mybir as mybir

BF16 = mybir.dt.bfloat16
F32 = mybir.dt.float32
U16 = mybir.dt.uint16
SIGMOID = mybir.ActivationFunctionType.Sigmoid
MULT = mybir.AluOpType.mult

P = 128
S = 2048
N = 384
M = 512
H = 256
PIECE = N // 2
DMA_BLOCK = 256
BANKS = 3
FIRST_BLOCK = 1
OTHER_BLOCK = 0

FLOPS = 2 * P * M * N


def tile_gather_matmul_kernel(tc, table, w, offs, out):
    nc = tc.nc
    blocks = range(H // P)
    pieces = range(N // PIECE)
    with (
        tc.tile_pool(name="held", bufs=1) as held,
        tc.tile_pool(name="work", bufs=len(blocks)) as work,
        tc.psum_pool(name="psum", bufs=len(blocks)) as psum,
    ):
        words = held.tile([P, S], BF16, name="words", align_bytes=DMA_BLOCK)
        nc.scalar.dma_start(words[:], table)
        first_weights = held.tile([P, P], BF16, name="first_weights", align_bytes=DMA_BLOCK)
        nc.sync.dma_start(first_weights[:], w[:, M - P : M])
        offsets = held.tile([P, N // 16], U16, name="offsets")
        nc.sync.dma_start(offsets[:], offs)
        other_weights = held.tile([P, M - P], BF16, name="other_weights", align_bytes=DMA_BLOCK)
        nc.scalar.dma_start(other_weights[:], w[:, 0 : M - P])

        def gate_weights(block):
            if block == FIRST_BLOCK:
                return first_weights[:]
            return other_weights[:, H + block * P : H + (block + 1) * P]

        early_in = held.tile([P, 1], F32, name="early_in")
        nc.vector.memset(early_in[:], 0.0)
        early_out = held.tile([P, 1], F32, name="early_out")
        nc.scalar.activation(early_out[:], early_in[:], SIGMOID)

        def make_gates(block, gate_pieces):
            first = gate_pieces[0] * PIECE
            width = len(gate_pieces) * PIECE
            gate_bank = psum.tile([P, width], F32, name="gate_bank", bufs=BANKS)
            nc.tensor.matmul(
                gate_bank[:],
                gate_weights(block),
                words[:].indirect(offsets[:, first // 16 : (first + width) // 16]),
                start=True,
                stop=True,
            )
            for place, piece in enumerate(gate_pieces):
                gate = work.tile([P, PIECE], F32, name="gate", bufs=len(blocks) * len(pieces))
                nc.scalar.activation(gate[:], gate_bank[:, place * PIECE : (place + 1) * PIECE], SIGMOID)
                gates[block, piece] = gate

        def make_output(block, value_pieces):
            rows = slice(block * P, (block + 1) * P)
            first = value_pieces[0] * PIECE
            width = len(value_pieces) * PIECE
            value_bank = psum.tile([P, width], F32, name="value_bank", bufs=BANKS)
            nc.tensor.matmul(
                value_bank[:],
                other_weights[:, rows],
                words[:].indirect(offsets[:, first // 16 : (first + width) // 16]),
                start=True,
                stop=True,
            )
            for place, piece in enumerate(value_pieces):
                gated = work.tile(
                    [P, PIECE], F32, name="gated", bufs=len(blocks) * len(pieces), align_bytes=DMA_BLOCK
                )
                nc.vector.tensor_tensor(
                    gated[:], value_bank[:, place * PIECE : (place + 1) * PIECE], gates[block, piece][:], MULT
                )
                nc.sync.dma_start(out[rows, piece * PIECE : (piece + 1) * PIECE], gated[:])

        gates = {}
        make_gates(FIRST_BLOCK, (0, 1))
        make_output(FIRST_BLOCK, (0, 1))
        make_gates(OTHER_BLOCK, (0,))
        make_gates(OTHER_BLOCK, (1,))
        make_output(OTHER_BLOCK, (0,))
        make_output(OTHER_BLOCK, (1,))
